import numpy as np
import ml_dtypes


def mxq(x, axis, fmt="e4m3"):
    dtype, down = {"e4m3": (ml_dtypes.float8_e4m3fn, 7), "e5m2": (ml_dtypes.float8_e5m2, 14)}[fmt]
    v = np.moveaxis(np.asarray(x, np.float32).astype(ml_dtypes.bfloat16).astype(np.float64), axis, -1)
    blocks = v.reshape(v.shape[:-1] + (-1, 32))
    amax = np.abs(blocks).max(-1, keepdims=True)
    byte = np.maximum(np.where(amax > 0, np.frexp(amax)[1] - 1 + 127, 0) - down, 1)
    scale = np.exp2(byte - 127.0)
    codes = (blocks / scale).astype(np.float32).astype(dtype).astype(np.float64)
    return np.moveaxis((codes * scale).reshape(v.shape), -1, axis)


WIDE = False


def mx_kscale(k):
    if not WIDE:
        return np.ones(k)
    levels = np.array([10, -10, 5, -5, 0])
    if k % 512:
        return np.exp2(np.random.permutation(np.resize(levels, k // 32))).repeat(32)
    a = np.empty((k // 512, 16))
    for p in range(k // 512):
        a[p, :8] = np.random.permutation(np.resize(levels, 8))
        for g in range(8):
            far = levels[np.abs(levels - a[p, g]) >= 10]
            a[p, g + 8] = far[np.random.randint(len(far))]
    return np.exp2(a.ravel()).repeat(32)


def f64(x):
    return np.asarray(x).astype(np.float64)


def striped(idx):
    return np.tile(idx.reshape(-1, 16).T, (8, 1)).astype(np.uint16)


def unstriped(offs):
    return offs[:16].T.reshape(-1).astype(np.int64)


def pack_weight(w):
    k, n = w.shape
    w = f64(np.asarray(w, np.float32).astype(ml_dtypes.bfloat16)).reshape(k // 32, 32, n)
    amax = np.abs(w).max(1)
    byte = np.clip(np.where(amax > 0, np.frexp(amax)[1] - 1 + 127 - 7, 1), 1, 254)
    scaled = (w * np.exp2(127.0 - byte)[:, None, :]).reshape(k, n).astype(np.float32)
    words = np.ascontiguousarray(scaled.reshape(k // 512, 128, 4, n).transpose(0, 1, 3, 2)).astype(ml_dtypes.float8_e4m3fn).view(np.uint8)
    return words, np.ascontiguousarray(byte.astype(np.uint8).reshape(k // 512, 16, n))


def unpack_weight(words, scales):
    g, p, n, _ = words.shape
    vals = np.ascontiguousarray(words).view(ml_dtypes.float8_e4m3fn).astype(np.float64) * np.repeat(np.exp2(scales.astype(np.float64) - 127.0), 8, axis=1)[..., None]
    return vals.transpose(0, 1, 3, 2).reshape(g * 512, n)


def silu(v):
    return v / (1.0 + np.exp(-np.maximum(v, -700.0)))


K, T, D, S, V, N = 1024, 1024, 4, 1024, 256, 128


def setup_inputs():
    n = np.random.standard_normal
    s = mx_kscale(K)[:, None]
    words, scales = pack_weight(n((K, N)) / np.sqrt(K) / s)
    return {
        "xT": (n((K, T)) * s / np.sqrt(D)).astype(ml_dtypes.bfloat16).astype(np.float32),
        "w_words": words,
        "w_scales": scales,
        "b": (0.3 * n((N, 1))).astype(np.float32),
        "offs": striped(np.concatenate([np.random.permutation(T)[:V] for _ in range(D)])),
    }


def reference(xT, w_words, w_scales, b, offs):
    w = unpack_weight(w_words, w_scales)
    idx = unstriped(offs)
    x = sum(f64(xT)[:, idx[d * V:(d + 1) * V]] for d in range(D))
    return silu((w.T @ mxq(x, 0, "e4m3")) + f64(b))

@@ -1,0 +1,226 @@
+from contextlib import ExitStack
+
+import concourse.mybir as mybir
+from concourse.masks import make_identity
+
+K, T, D, V, N = 1024, 1024, 4, 256, 128
+FLOPS = 2 * K * N * V
+
+F32 = mybir.dt.float32
+BF16 = mybir.dt.bfloat16
+I32 = mybir.dt.int32
+U32 = mybir.dt.uint32
+U16 = mybir.dt.uint16
+U8 = mybir.dt.uint8
+FP8X4 = mybir.dt.float8_e4m3fn_x4
+ACT = mybir.ActivationFunctionType
+
+P = 128
+PACK = 4
+PASSES = K // (P * PACK)
+HALF = 128
+HALVES = V // HALF
+GROUP = 16
+
+
+def tile_picked_hash_lin_silu_sub_l_kernel(tc, xT, w_words, w_scales, b, offs, out):
+    nc = tc.nc
+    with ExitStack() as ctx:
+        keep = ctx.enter_context(tc.tile_pool(name="keep", bufs=1))
+        shared = ctx.enter_context(tc.tile_pool(name="shared", bufs=1))
+        psum = ctx.enter_context(tc.psum_pool(name="psum", bufs=1))
+
+        offsets = keep.tile([P, D * V // GROUP], U16, name="offsets")
+        rows = xT.rearrange("(a p t) n -> a t p n", p=P, t=PACK)
+        arrival = [(a, t) for a in range(PASSES) for t in (0, 2, 1, 3)]
+        row_bytes = 4 * T
+        place = {plane: i * row_bytes for i, plane in enumerate(arrival)}
+        spare = len(arrival) * row_bytes
+
+        def placed(shape, dtype, name, at):
+            return shared.tile(shape, dtype, name=name, offset=at, align_bytes=64)
+
+        table = {}
+        for i, (a, t) in enumerate(arrival):
+            table[a, t] = placed([P, T], F32, "table_%d_%d" % (a, t), place[a, t])
+            if i == 0:
+                nc.sync.dma_start(table[a, t][:, : T // 2], rows[a, t][:, : T // 2])
+                nc.sync.dma_start(offsets[:], offs)
+                nc.sync.dma_start(table[a, t][:, T // 2 :], rows[a, t][:, T // 2 :])
+            else:
+                nc.sync.dma_start(table[a, t][:], rows[a, t])
+
+        w_codes = keep.tile([P, PASSES, N], U32, name="w_codes", align_bytes=64)
+        w_plane = keep.tile([P, PASSES, N], U8, name="w_plane", align_bytes=64)
+        bias = keep.tile([P, 1], F32, name="bias")
+        widened = [keep.tile([P, D * V], F32, name="widened_%d" % e) for e in range(2)]
+        for e in range(2):
+            nc.vector.memset(widened[e][:].bitcast(I32), 0)
+        nc.vector.memset(w_plane[:].rearrange("p a m -> p (a m)").bitcast(I32), 0)
+        nc.sync.dma_start(
+            w_codes[:].bitcast(I32), w_words.rearrange("a p m r -> p a (m r)").bitcast(I32)
+        )
+        nc.sync.dma_start(bias[:], b)
+        for q in range(4):
+            nc.sync.dma_start(
+                w_plane[32 * q : 32 * q + 4].bitcast(I32),
+                w_scales[:, 4 * q : 4 * q + 4, :].rearrange("a r m -> r a m").bitcast(I32),
+            )
+
+        identity = keep.tile([P, P], F32, name="identity")
+        make_identity(nc, identity[:])
+        warm_in = keep.tile([P, 1], F32, name="warm_in")
+        warm_out = keep.tile([P, 1], F32, name="warm_out")
+        nc.vector.memset(warm_in[:], 0.0)
+        nc.scalar.activation(warm_out[:], warm_in[:], ACT.Silu)
+
+        def list_slice(first, width):
+            return offsets[:, first // GROUP : (first + width) // GROUP]
+
+        def narrow(plane, cuts=1):
+            small = keep.tile([P, T], BF16, name="small_%d_%d" % plane)
+            for c in range(cuts):
+                cols = slice(c * T // cuts, (c + 1) * T // cuts)
+                nc.vector.tensor_copy(small[:, cols], table[plane][:, cols])
+            return small
+
+        def blocks(picked, first, width):
+            return {first + j: picked[:, j : j + HALF] for j in range(0, width, HALF)}
+
+        def gather_scalar(small, e, first, width):
+            halves = widened[e][:].bitcast(BF16)
+            nc.scalar.activation(
+                halves[:, 2 * first + 1 : 2 * (first + width) : 2],
+                small[:].indirect(list_slice(first, width)),
+                ACT.Copy,
+            )
+            return blocks(widened[e][:, first : first + width], first, width)
+
+        def gather_vector(plane, first, width, at=None):
+            name = "picked_%d_%d_%d" % (plane + (first,))
+            if at is None:
+                picked = keep.tile([P, width], F32, name=name)
+            else:
+                picked = placed([P, width], F32, name, at)
+            nc.vector.tensor_copy(picked[:], table[plane][:].indirect(list_slice(first, width)))
+            return blocks(picked[:], first, width)
+
+        def add_up(found, h, dest):
+            for d in range(D):
+                nc.tensor.matmul(
+                    dest, lhsT=found[d * V + h * HALF], rhs=identity[:],
+                    is_transpose=True, start=(d == 0), stop=(d == D - 1),
+                )
+
+        def round_pairs(copy, sums, name, at=None):
+            count = sums.shape[1]
+            if at is None:
+                pairs = keep.tile([P, count, P, 2], BF16, name=name)
+            else:
+                pairs = placed([P, count, P, 2], BF16, name, at)
+            copy(pairs[:], sums.rearrange("v h e p -> v h p e"))
+            return pairs[:].rearrange("v h p e -> v h (p e)").bitcast(F32)
+
+        def interleave(copy, turned, name):
+            grouped = keep.tile([P, turned.shape[2] * PACK], BF16, name=name, align_bytes=64)
+            copy(grouped[:].bitcast(F32).rearrange("p (v u) -> p v u", u=2), turned.rearrange("p u v -> p v u"))
+            return grouped
+
+        def quantise(grouped, codes, plane):
+            nc.vector.quantize_mx(out=codes[:].bitcast(FP8X4), scales=plane[:], in_=grouped[:])
+
+        sums00 = psum.tile([P, HALVES, 2, P], F32, name="sums00", tag="early0")
+        sums01 = psum.tile([P, HALVES, 2, P], F32, name="sums01", tag="early1")
+        sums10 = psum.tile([P, HALVES, 2, P], F32, name="sums10")
+        sums11 = [psum.tile([P, 1, 2, P], F32, name="sums11_%d" % h) for h in range(HALVES)]
+        turned0 = psum.tile([P, 2, V], F32, name="turned0")
+        turned1 = [psum.tile([P, 2, HALF], F32, name="turned1_%d" % h) for h in range(HALVES)]
+
+        def both_halves(found, sums, e):
+            for h in range(HALVES):
+                add_up(found, h, sums[:, h, e, :])
+
+        def turn(words, turned, u):
+            for h in range(HALVES):
+                nc.tensor.transpose(turned[h][:, u, :], words[:, h, :], identity[:])
+
+        turned0_halves = [turned0[:, :, h * HALF : (h + 1) * HALF] for h in range(HALVES)]
+        by_half = [[d * V + h * HALF for d in range(D)] for h in range(HALVES)]
+
+        small = narrow((0, 0), cuts=2)
+        found = {}
+        for d in range(D):
+            found.update(gather_scalar(small, 0, d * V, V))
+        both_halves(found, sums00, 0)
+        found = gather_vector((0, 2), 0, 2 * V)
+        small = narrow((0, 1))
+        found.update(gather_vector((0, 2), 2 * V, 2 * V, at=place[0, 1]))
+        both_halves(found, sums01, 0)
+
+        found = {}
+        for d in range(D):
+            found.update(gather_scalar(small, 1, d * V, V))
+        both_halves(found, sums00, 1)
+        found = gather_vector((0, 3), 0, V)
+        small = narrow((1, 0))
+        found.update(gather_vector((0, 3), V, V, at=place[1, 0]))
+        found.update(gather_vector((0, 3), 2 * V, 2 * V, at=place[1, 0] + 4 * V))
+        both_halves(found, sums01, 1)
+
+        found = gather_scalar(small, 0, 0, V)
+        words00 = round_pairs(nc.scalar.copy, sums00[:], "pairs00", at=place[1, 0] + 12 * V)
+        for d in range(1, D):
+            found.update(gather_scalar(small, 0, d * V, V))
+        turn(words00, turned0_halves, 0)
+        both_halves(found, sums10, 0)
+
+        small = narrow((1, 1))
+        found = gather_vector((1, 2), 0, 2 * V, at=place[1, 1])
+        found.update(gather_vector((1, 2), 2 * V, 2 * V, at=place[1, 1] + 8 * V))
+        for h in range(HALVES):
+            add_up(found, h, sums11[h][:, 0, 0, :])
+        for h in range(HALVES):
+            found = {}
+            for first in by_half[h]:
+                found.update(gather_scalar(small, 1, first, HALF))
+            add_up(found, h, sums10[:, h, 1, :])
+
+        found = {}
+        for d, first in enumerate(by_half[0]):
+            found.update(gather_vector((1, 3), first, HALF, at=spare + 4 * HALF * d))
+        add_up(found, 0, sums11[0][:, 0, 1, :])
+        words01 = round_pairs(nc.scalar.copy, sums01[:], "pairs01", at=spare)
+        words10 = round_pairs(nc.scalar.copy, sums10[:], "pairs10", at=spare + 8 * HALF)
+        turn(words01, turned0_halves, 1)
+        found = {}
+        for first in by_half[1]:
+            found.update(gather_vector((1, 3), first, HALF))
+        turn(words10, turned1, 0)
+        add_up(found, 1, sums11[1][:, 0, 1, :])
+        grouped0 = interleave(nc.scalar.copy, turned0[:], "grouped0")
+        codes0 = placed([P, V], U32, "codes0", place[1, 3])
+        plane0 = placed([P, V], U8, "plane0", place[1, 3] + 4 * V)
+        quantise(grouped0, codes0, plane0)
+
+        copies = [nc.scalar.copy, nc.vector.tensor_copy]
+        words11 = [round_pairs(copies[h], sums11[h][:], "pairs11_%d" % h) for h in range(HALVES)]
+        for h in range(HALVES):
+            nc.tensor.transpose(turned1[h][:, 1, :], words11[h][:, 0, :], identity[:])
+        for h in range(HALVES):
+            grouped1 = interleave(copies[h], turned1[h][:], "grouped1_%d" % h)
+            codes1 = keep.tile([P, HALF], U32, name="codes1_%d" % h, align_bytes=64)
+            plane1 = keep.tile([P, HALF], U8, name="plane1_%d" % h, align_bytes=64)
+            quantise(grouped1, codes1, plane1)
+            acc = psum.tile([N, HALF], F32, name="acc_%d" % h, tag="early%d" % h)
+            cols = slice(h * HALF, (h + 1) * HALF)
+            nc.tensor.matmul_mx(
+                out=acc[:], lhsT=w_codes[:, 0, :].bitcast(FP8X4), lhsT_scale=w_plane[:, 0, :],
+                rhs=codes0[:, cols].bitcast(FP8X4), rhs_scale=plane0[:, cols], start=True, stop=False,
+            )
+            nc.tensor.matmul_mx(
+                out=acc[:], lhsT=w_codes[:, 1, :].bitcast(FP8X4), lhsT_scale=w_plane[:, 1, :],
+                rhs=codes1[:].bitcast(FP8X4), rhs_scale=plane1[:], start=False, stop=True,
+            )
+            result = keep.tile([N, HALF], F32, name="result_%d" % h)
+            nc.scalar.activation(result[:], acc[:], ACT.Silu, bias=bias[:])
+            nc.sync.dma_start(out[:, cols], result[:])

@@ -32,10 +32,11 @@ def tile_picked_hash_lin_silu_sub_l_kernel(tc, xT, w_words, w_scales, b, offs, o
 
         offsets = keep.tile([P, D * V // GROUP], U16, name="offsets")
         rows = xT.rearrange("(a p t) n -> a t p n", p=P, t=PACK)
-        arrival = [(a, t) for a in range(PASSES) for t in (0, 2, 1, 3)]
+        arrival = [(0, 0), (0, 1), (0, 2), (1, 0), (0, 3), (1, 2), (1, 1), (1, 3)]
         row_bytes = 4 * T
         place = {plane: i * row_bytes for i, plane in enumerate(arrival)}
-        spare = len(arrival) * row_bytes
+        place["small"] = len(arrival) * row_bytes
+        spare = (len(arrival) + 1) * row_bytes
 
         def placed(shape, dtype, name, at):
             return shared.tile(shape, dtype, name=name, offset=at, align_bytes=64)
@@ -54,9 +55,8 @@ def tile_picked_hash_lin_silu_sub_l_kernel(tc, xT, w_words, w_scales, b, offs, o
         w_plane = keep.tile([P, PASSES, N], U8, name="w_plane", align_bytes=64)
         bias = keep.tile([P, 1], F32, name="bias")
         widened = [keep.tile([P, D * V], F32, name="widened_%d" % e) for e in range(2)]
-        for e in range(2):
-            nc.vector.memset(widened[e][:].bitcast(I32), 0)
-        nc.vector.memset(w_plane[:].rearrange("p a m -> p (a m)").bitcast(I32), 0)
+        nc.vector.memset(widened[0][:].bitcast(I32), 0)
+        nc.gpsimd.memset(w_plane[:].rearrange("p a m -> p (a m)").bitcast(I32), 0)
         nc.sync.dma_start(
             w_codes[:].bitcast(I32), w_words.rearrange("a p m r -> p a (m r)").bitcast(I32)
         )
@@ -69,6 +69,7 @@ def tile_picked_hash_lin_silu_sub_l_kernel(tc, xT, w_words, w_scales, b, offs, o
 
         identity = keep.tile([P, P], F32, name="identity")
         make_identity(nc, identity[:])
+        nc.gpsimd.memset(widened[1][:].bitcast(I32), 0)
         warm_in = keep.tile([P, 1], F32, name="warm_in")
         warm_out = keep.tile([P, 1], F32, name="warm_out")
         nc.vector.memset(warm_in[:], 0.0)
@@ -77,11 +78,14 @@ def tile_picked_hash_lin_silu_sub_l_kernel(tc, xT, w_words, w_scales, b, offs, o
         def list_slice(first, width):
             return offsets[:, first // GROUP : (first + width) // GROUP]
 
-        def narrow(plane, cuts=1):
-            small = keep.tile([P, T], BF16, name="small_%d_%d" % plane)
+        def narrow(plane, cuts=1, at=None, copy=nc.vector.tensor_copy):
+            if at is None:
+                small = keep.tile([P, T], BF16, name="small_%d_%d" % plane)
+            else:
+                small = placed([P, T], BF16, "small_%d_%d" % plane, at)
             for c in range(cuts):
                 cols = slice(c * T // cuts, (c + 1) * T // cuts)
-                nc.vector.tensor_copy(small[:, cols], table[plane][:, cols])
+                copy(small[:, cols], table[plane][:, cols])
             return small
 
         def blocks(picked, first, width):
@@ -105,11 +109,11 @@ def tile_picked_hash_lin_silu_sub_l_kernel(tc, xT, w_words, w_scales, b, offs, o
             nc.vector.tensor_copy(picked[:], table[plane][:].indirect(list_slice(first, width)))
             return blocks(picked[:], first, width)
 
-        def add_up(found, h, dest):
-            for d in range(D):
+        def add_up(found, h, dest, order):
+            for i, d in enumerate(order):
                 nc.tensor.matmul(
                     dest, lhsT=found[d * V + h * HALF], rhs=identity[:],
-                    is_transpose=True, start=(d == 0), stop=(d == D - 1),
+                    is_transpose=True, start=(i == 0), stop=(i == D - 1),
                 )
 
         def round_pairs(copy, sums, name, at=None):
@@ -129,89 +133,85 @@ def tile_picked_hash_lin_silu_sub_l_kernel(tc, xT, w_words, w_scales, b, offs, o
         def quantise(grouped, codes, plane):
             nc.vector.quantize_mx(out=codes[:].bitcast(FP8X4), scales=plane[:], in_=grouped[:])
 
-        sums00 = psum.tile([P, HALVES, 2, P], F32, name="sums00", tag="early0")
-        sums01 = psum.tile([P, HALVES, 2, P], F32, name="sums01", tag="early1")
-        sums10 = psum.tile([P, HALVES, 2, P], F32, name="sums10")
+        sums00 = psum.tile([P, HALVES, 2, P], F32, name="sums00", tag="bank_a")
+        sums01 = psum.tile([P, HALVES, 2, P], F32, name="sums01", tag="bank_b")
+        sums10 = [psum.tile([P, 1, 2, P], F32, name="sums10_%d" % h, tag="bank_c%d" % h) for h in range(HALVES)]
         sums11 = [psum.tile([P, 1, 2, P], F32, name="sums11_%d" % h) for h in range(HALVES)]
-        turned0 = psum.tile([P, 2, V], F32, name="turned0")
         turned1 = [psum.tile([P, 2, HALF], F32, name="turned1_%d" % h) for h in range(HALVES)]
 
-        def both_halves(found, sums, e):
+        def one_bank(found, sums, e, order=range(D)):
             for h in range(HALVES):
-                add_up(found, h, sums[:, h, e, :])
+                add_up(found, h, sums[:, h, e, :], order)
 
-        def turn(words, turned, u):
-            for h in range(HALVES):
-                nc.tensor.transpose(turned[h][:, u, :], words[:, h, :], identity[:])
+        def two_banks(found, sums, e):
+            for d in range(D):
+                for h in range(HALVES):
+                    nc.tensor.matmul(
+                        sums[h][:, 0, e, :], lhsT=found[d * V + h * HALF], rhs=identity[:],
+                        is_transpose=True, start=(d == 0), stop=(d == D - 1),
+                    )
 
-        turned0_halves = [turned0[:, :, h * HALF : (h + 1) * HALF] for h in range(HALVES)]
-        by_half = [[d * V + h * HALF for d in range(D)] for h in range(HALVES)]
-
-        small = narrow((0, 0), cuts=2)
-        found = {}
-        for d in range(D):
-            found.update(gather_scalar(small, 0, d * V, V))
-        both_halves(found, sums00, 0)
-        found = gather_vector((0, 2), 0, 2 * V)
-        small = narrow((0, 1))
-        found.update(gather_vector((0, 2), 2 * V, 2 * V, at=place[0, 1]))
-        both_halves(found, sums01, 0)
-
-        found = {}
-        for d in range(D):
-            found.update(gather_scalar(small, 1, d * V, V))
-        both_halves(found, sums00, 1)
-        found = gather_vector((0, 3), 0, V)
-        small = narrow((1, 0))
-        found.update(gather_vector((0, 3), V, V, at=place[1, 0]))
-        found.update(gather_vector((0, 3), 2 * V, 2 * V, at=place[1, 0] + 4 * V))
-        both_halves(found, sums01, 1)
-
-        found = gather_scalar(small, 0, 0, V)
-        words00 = round_pairs(nc.scalar.copy, sums00[:], "pairs00", at=place[1, 0] + 12 * V)
-        for d in range(1, D):
-            found.update(gather_scalar(small, 0, d * V, V))
-        turn(words00, turned0_halves, 0)
-        both_halves(found, sums10, 0)
-
-        small = narrow((1, 1))
-        found = gather_vector((1, 2), 0, 2 * V, at=place[1, 1])
-        found.update(gather_vector((1, 2), 2 * V, 2 * V, at=place[1, 1] + 8 * V))
-        for h in range(HALVES):
-            add_up(found, h, sums11[h][:, 0, 0, :])
-        for h in range(HALVES):
+        def scalar_pieces(small, e, count):
             found = {}
-            for first in by_half[h]:
-                found.update(gather_scalar(small, 1, first, HALF))
-            add_up(found, h, sums10[:, h, 1, :])
+            for d in range(count):
+                found.update(gather_scalar(small, e, d * V, V))
+            return found
 
-        found = {}
-        for d, first in enumerate(by_half[0]):
-            found.update(gather_vector((1, 3), first, HALF, at=spare + 4 * HALF * d))
-        add_up(found, 0, sums11[0][:, 0, 1, :])
-        words01 = round_pairs(nc.scalar.copy, sums01[:], "pairs01", at=spare)
-        words10 = round_pairs(nc.scalar.copy, sums10[:], "pairs10", at=spare + 8 * HALF)
-        turn(words01, turned0_halves, 1)
-        found = {}
-        for first in by_half[1]:
-            found.update(gather_vector((1, 3), first, HALF))
-        turn(words10, turned1, 0)
-        add_up(found, 1, sums11[1][:, 0, 1, :])
-        grouped0 = interleave(nc.scalar.copy, turned0[:], "grouped0")
-        codes0 = placed([P, V], U32, "codes0", place[1, 3])
-        plane0 = placed([P, V], U8, "plane0", place[1, 3] + 4 * V)
-        quantise(grouped0, codes0, plane0)
+        def vector_pieces(plane, widths, first=0, at=None):
+            found = {}
+            for width in widths:
+                found.update(gather_vector(plane, first, width, at))
+                first += width
+                at = None if at is None else at + 4 * width
+            return found
 
-        copies = [nc.scalar.copy, nc.vector.tensor_copy]
-        words11 = [round_pairs(copies[h], sums11[h][:], "pairs11_%d" % h) for h in range(HALVES)]
+        for e in range(2):
+            small = narrow((0, e), cuts=2 - e)
+            found = vector_pieces((0, e), [V], first=(D - 1) * V)
+            found.update(scalar_pieces(small, e, D - 1))
+            one_bank(found, sums00, e, order=(3, 0, 1, 2))
+        one_bank(vector_pieces((0, 2), [2 * V, 2 * V]), sums01, 0)
+        small = narrow((1, 0), copy=nc.scalar.copy)
+        two_banks(scalar_pieces(small, 0, D), sums10, 0)
+        one_bank(vector_pieces((0, 3), [2 * V, 2 * V]), sums01, 1)
+        found = vector_pieces((1, 2), [V])
+        small = narrow((1, 1), at=place["small"])
+        found.update(vector_pieces((1, 2), [3 * V], first=V, at=place[1, 1]))
+        two_banks(found, sums11, 0)
+        two_banks(scalar_pieces(small, 1, D), sums10, 1)
+        two_banks(vector_pieces((1, 3), [2 * V, V, HALF, HALF], at=spare), sums11, 1)
+
+        late_identity = placed([P, P], F32, "late_identity", spare)
+        nc.gpsimd.tensor_copy(late_identity[:], identity[:])
+        words00 = round_pairs(nc.scalar.copy, sums00[:], "pairs00", at=place["small"])
+        words01 = round_pairs(nc.scalar.copy, sums01[:], "pairs01", at=place["small"] + 4 * V)
+        words10 = [
+            round_pairs(nc.scalar.copy, sums10[h][:], "pairs10_%d" % h, at=spare + 8 * V + 2 * V * h)
+            for h in range(HALVES)
+        ]
+        words11 = [
+            round_pairs(nc.vector.tensor_copy, sums11[h][:], "pairs11_%d" % h, at=place[1, 3] + 2 * V * h)
+            for h in range(HALVES)
+        ]
+        turned0 = psum.tile([P, 2, V], F32, name="turned0", tag="bank_a")
+        for u, words in enumerate((words00, words01)):
+            for h in range(HALVES):
+                nc.tensor.transpose(turned0[:, u, h * HALF : (h + 1) * HALF], words[:, h, :], late_identity[:])
         for h in range(HALVES):
+            nc.tensor.transpose(turned1[h][:, 0, :], words10[h][:, 0, :], identity[:])
             nc.tensor.transpose(turned1[h][:, 1, :], words11[h][:, 0, :], identity[:])
+        grouped0 = interleave(nc.scalar.copy, turned0[:], "grouped0")
+        copies = [nc.scalar.copy, nc.vector.tensor_copy]
+        grouped = [interleave(copies[h], turned1[h][:], "grouped1_%d" % h) for h in range(HALVES)]
+        codes0 = keep.tile([P, V], U32, name="codes0", align_bytes=64)
+        plane0 = keep.tile([P, V], U8, name="plane0", align_bytes=64)
+        quantise(grouped0, codes0, plane0)
         for h in range(HALVES):
-            grouped1 = interleave(copies[h], turned1[h][:], "grouped1_%d" % h)
+            grouped1 = grouped[h]
             codes1 = keep.tile([P, HALF], U32, name="codes1_%d" % h, align_bytes=64)
             plane1 = keep.tile([P, HALF], U8, name="plane1_%d" % h, align_bytes=64)
             quantise(grouped1, codes1, plane1)
-            acc = psum.tile([N, HALF], F32, name="acc_%d" % h, tag="early%d" % h)
+            acc = psum.tile([N, HALF], F32, name="acc_%d" % h, tag=("bank_b", "bank_c0")[h])
             cols = slice(h * HALF, (h + 1) * HALF)
             nc.tensor.matmul_mx(
                 out=acc[:], lhsT=w_codes[:, 0, :].bitcast(FP8X4), lhsT_scale=w_plane[:, 0, :],

@@ -25,31 +25,31 @@ GROUP = 16
 
 def tile_picked_hash_lin_silu_sub_l_kernel(tc, xT, w_words, w_scales, b, offs, out):
     nc = tc.nc
+    add = mybir.AluOpType.add
     with ExitStack() as ctx:
         keep = ctx.enter_context(tc.tile_pool(name="keep", bufs=1))
         shared = ctx.enter_context(tc.tile_pool(name="shared", bufs=1))
         psum = ctx.enter_context(tc.psum_pool(name="psum", bufs=1))
 
-        offsets = keep.tile([P, D * V // GROUP], U16, name="offsets")
-        rows = xT.rearrange("(a p t) n -> a t p n", p=P, t=PACK)
-        arrival = [(0, 0), (0, 1), (0, 2), (1, 0), (0, 3), (1, 2), (1, 1), (1, 3)]
-        row_bytes = 4 * T
-        place = {plane: i * row_bytes for i, plane in enumerate(arrival)}
-        place["small"] = len(arrival) * row_bytes
-        spare = (len(arrival) + 1) * row_bytes
-
         def placed(shape, dtype, name, at):
             return shared.tile(shape, dtype, name=name, offset=at, align_bytes=64)
 
-        table = {}
-        for i, (a, t) in enumerate(arrival):
-            table[a, t] = placed([P, T], F32, "table_%d_%d" % (a, t), place[a, t])
-            if i == 0:
-                nc.sync.dma_start(table[a, t][:, : T // 2], rows[a, t][:, : T // 2])
-                nc.sync.dma_start(offsets[:], offs)
-                nc.sync.dma_start(table[a, t][:, T // 2 :], rows[a, t][:, T // 2 :])
-            else:
-                nc.sync.dma_start(table[a, t][:], rows[a, t])
+        offsets = keep.tile([P, D * V // GROUP], U16, name="offsets")
+        rows = xT.rearrange("(a p t) n -> a p t n", p=P, t=PACK)
+        left, right = slice(0, T // 2), slice(T // 2, T)
+        most, rest = slice(0, 3 * T // 4), slice(3 * T // 4, T)
+        single = [keep.tile([P, T], F32, name="single_%d" % t) for t in range(PACK)]
+        double = [keep.tile([P, 2, T], F32, name="double_%d" % u) for u in range(2)]
+        nc.sync.dma_start(single[0][:, most], rows[0, :, 0, most])
+        nc.sync.dma_start(offsets[:], offs)
+        nc.sync.dma_start(single[0][:, rest], rows[0, :, 0, rest])
+        nc.sync.dma_start(single[1][:], rows[0, :, 1, :])
+        nc.sync.dma_start(double[0][:, :, left], rows[1, :, 0:2, left])
+        nc.sync.dma_start(double[0][:, :, right], rows[1, :, 0:2, right])
+        nc.sync.dma_start(single[2][:], rows[0, :, 2, :])
+        nc.sync.dma_start(single[3][:], rows[0, :, 3, :])
+        nc.sync.dma_start(double[1][:, :, left], rows[1, :, 2:4, left])
+        nc.sync.dma_start(double[1][:, :, right], rows[1, :, 2:4, right])
 
         w_codes = keep.tile([P, PASSES, N], U32, name="w_codes", align_bytes=64)
         w_plane = keep.tile([P, PASSES, N], U8, name="w_plane", align_bytes=64)
@@ -78,149 +78,143 @@ def tile_picked_hash_lin_silu_sub_l_kernel(tc, xT, w_words, w_scales, b, offs, o
         def list_slice(first, width):
             return offsets[:, first // GROUP : (first + width) // GROUP]
 
-        def narrow(plane, cuts=1, at=None, copy=nc.vector.tensor_copy):
-            if at is None:
-                small = keep.tile([P, T], BF16, name="small_%d_%d" % plane)
-            else:
-                small = placed([P, T], BF16, "small_%d_%d" % plane, at)
-            for c in range(cuts):
-                cols = slice(c * T // cuts, (c + 1) * T // cuts)
-                copy(small[:, cols], table[plane][:, cols])
-            return small
+        small = [keep.tile([P, T], BF16, name="small_%d" % t) for t in range(PACK - 1)]
+        small.append(placed([P, T], BF16, "small_last", 0))
 
-        def blocks(picked, first, width):
-            return {first + j: picked[:, j : j + HALF] for j in range(0, width, HALF)}
+        def narrow(copy, t, cols):
+            copy(small[t][:, cols], single[t][:, cols])
 
-        def gather_scalar(small, e, first, width):
-            halves = widened[e][:].bitcast(BF16)
+        def gather_scalar(t, d):
+            dest = widened[t % 2]
             nc.scalar.activation(
-                halves[:, 2 * first + 1 : 2 * (first + width) : 2],
-                small[:].indirect(list_slice(first, width)),
+                dest[:].bitcast(BF16)[:, 2 * d * V + 1 : 2 * (d + 1) * V : 2],
+                small[t][:].indirect(list_slice(d * V, V)),
                 ACT.Copy,
             )
-            return blocks(widened[e][:, first : first + width], first, width)
+            return dest[:, d * V : (d + 1) * V]
 
-        def gather_vector(plane, first, width, at=None):
-            name = "picked_%d_%d_%d" % (plane + (first,))
-            if at is None:
-                picked = keep.tile([P, width], F32, name=name)
-            else:
-                picked = placed([P, width], F32, name, at)
-            nc.vector.tensor_copy(picked[:], table[plane][:].indirect(list_slice(first, width)))
-            return blocks(picked[:], first, width)
+        def gather_vector(t, d):
+            picked = keep.tile([P, V], F32, name="picked_%d" % t)
+            nc.vector.tensor_copy(picked[:], single[t][:].indirect(list_slice(d * V, V)))
+            return picked[:]
 
-        def add_up(found, h, dest, order):
-            for i, d in enumerate(order):
-                nc.tensor.matmul(
-                    dest, lhsT=found[d * V + h * HALF], rhs=identity[:],
-                    is_transpose=True, start=(i == 0), stop=(i == D - 1),
-                )
+        def add_turned(dest, piece, h, i):
+            nc.tensor.matmul(
+                dest, lhsT=piece[:, h * HALF : (h + 1) * HALF], rhs=identity[:],
+                is_transpose=True, start=(i == 0), stop=(i == D - 1),
+            )
 
-        def round_pairs(copy, sums, name, at=None):
-            count = sums.shape[1]
-            if at is None:
-                pairs = keep.tile([P, count, P, 2], BF16, name=name)
-            else:
-                pairs = placed([P, count, P, 2], BF16, name, at)
-            copy(pairs[:], sums.rearrange("v h e p -> v h p e"))
-            return pairs[:].rearrange("v h p e -> v h (p e)").bitcast(F32)
+        sums_low = psum.tile([P, HALVES, 2, P], F32, name="sums_low")
+        sums_high = [psum.tile([P, 2, P], F32, name="sums_high_%d" % h) for h in range(HALVES)]
+        turned = [psum.tile([P, 2, HALF], F32, name="turned_%d" % h) for h in range(HALVES)]
+        acc = [psum.tile([N, HALF], F32, name="acc_%d" % h) for h in range(HALVES)]
 
-        def interleave(copy, turned, name):
-            grouped = keep.tile([P, turned.shape[2] * PACK], BF16, name=name, align_bytes=64)
-            copy(grouped[:].bitcast(F32).rearrange("p (v u) -> p v u", u=2), turned.rearrange("p u v -> p v u"))
-            return grouped
-
-        def quantise(grouped, codes, plane):
-            nc.vector.quantize_mx(out=codes[:].bitcast(FP8X4), scales=plane[:], in_=grouped[:])
-
-        sums00 = psum.tile([P, HALVES, 2, P], F32, name="sums00", tag="bank_a")
-        sums01 = psum.tile([P, HALVES, 2, P], F32, name="sums01", tag="bank_b")
-        sums10 = [psum.tile([P, 1, 2, P], F32, name="sums10_%d" % h, tag="bank_c%d" % h) for h in range(HALVES)]
-        sums11 = [psum.tile([P, 1, 2, P], F32, name="sums11_%d" % h) for h in range(HALVES)]
-        turned1 = [psum.tile([P, 2, HALF], F32, name="turned1_%d" % h) for h in range(HALVES)]
-
-        def one_bank(found, sums, e, order=range(D)):
+        def low_plane(t):
+            pieces = [gather_vector(t, D - 1)] + [gather_scalar(t, d) for d in range(D - 1)]
             for h in range(HALVES):
-                add_up(found, h, sums[:, h, e, :], order)
+                for i, piece in enumerate(pieces):
+                    add_turned(sums_low[:, h, t, :], piece, h, i)
 
-        def two_banks(found, sums, e):
+        def high_plane(t):
             for d in range(D):
+                piece = gather_scalar(t, d)
                 for h in range(HALVES):
-                    nc.tensor.matmul(
-                        sums[h][:, 0, e, :], lhsT=found[d * V + h * HALF], rhs=identity[:],
-                        is_transpose=True, start=(d == 0), stop=(d == D - 1),
-                    )
+                    add_turned(sums_high[h][:, t - 2, :], piece, h, d)
 
-        def scalar_pieces(small, e, count):
-            found = {}
-            for d in range(count):
-                found.update(gather_scalar(small, e, d * V, V))
-            return found
+        paired = [keep.tile([P, T], U32, name="paired_%d" % u) for u in range(2)]
+        partial = [placed([P, 2, 2 * V], F32, "partial_%d" % j, 2 * T + j * 16 * V) for j in range(2)]
 
-        def vector_pieces(plane, widths, first=0, at=None):
-            found = {}
-            for width in widths:
-                found.update(gather_vector(plane, first, width, at))
-                first += width
-                at = None if at is None else at + 4 * width
-            return found
+        def pair_up(u, cols):
+            nc.vector.tensor_copy(
+                paired[u][:, cols].bitcast(BF16).rearrange("p (n e) -> p n e", e=2),
+                double[u][:, :, cols].rearrange("p e n -> p n e"),
+            )
 
-        for e in range(2):
-            small = narrow((0, e), cuts=2 - e)
-            found = vector_pieces((0, e), [V], first=(D - 1) * V)
-            found.update(scalar_pieces(small, e, D - 1))
-            one_bank(found, sums00, e, order=(3, 0, 1, 2))
-        one_bank(vector_pieces((0, 2), [2 * V, 2 * V]), sums01, 0)
-        small = narrow((1, 0), copy=nc.scalar.copy)
-        two_banks(scalar_pieces(small, 0, D), sums10, 0)
-        one_bank(vector_pieces((0, 3), [2 * V, 2 * V]), sums01, 1)
-        found = vector_pieces((1, 2), [V])
-        small = narrow((1, 1), at=place["small"])
-        found.update(vector_pieces((1, 2), [3 * V], first=V, at=place[1, 1]))
-        two_banks(found, sums11, 0)
-        two_banks(scalar_pieces(small, 1, D), sums10, 1)
-        two_banks(vector_pieces((1, 3), [2 * V, V, HALF, HALF], at=spare), sums11, 1)
+        def gather_pairs(u, j):
+            words = keep.tile([P, 2 * V], U32, name="words_%d_%d" % (u, j))
+            nc.vector.tensor_copy(words[:], paired[u][:].indirect(list_slice(2 * j * V, 2 * V)))
+            return words[:].bitcast(BF16)
 
-        late_identity = placed([P, P], F32, "late_identity", spare)
-        nc.gpsimd.tensor_copy(late_identity[:], identity[:])
-        words00 = round_pairs(nc.scalar.copy, sums00[:], "pairs00", at=place["small"])
-        words01 = round_pairs(nc.scalar.copy, sums01[:], "pairs01", at=place["small"] + 4 * V)
-        words10 = [
-            round_pairs(nc.scalar.copy, sums10[h][:], "pairs10_%d" % h, at=spare + 8 * V + 2 * V * h)
-            for h in range(HALVES)
-        ]
-        words11 = [
-            round_pairs(nc.vector.tensor_copy, sums11[h][:], "pairs11_%d" % h, at=place[1, 3] + 2 * V * h)
-            for h in range(HALVES)
-        ]
-        turned0 = psum.tile([P, 2, V], F32, name="turned0", tag="bank_a")
-        for u, words in enumerate((words00, words01)):
+        def add_two(u, j, values, ids):
+            cols = slice(2 * ids.start, 2 * ids.stop)
+            nc.vector.tensor_tensor(
+                partial[j][:, u, cols], values[:, : 2 * V][:, cols], values[:, 2 * V :][:, cols], add
+            )
+
+        every = slice(0, V)
+        halves = [slice(h * HALF, (h + 1) * HALF) for h in range(HALVES)]
+
+        narrow(nc.vector.tensor_copy, 0, most)
+        narrow(nc.vector.tensor_copy, 0, rest)
+        low_plane(0)
+        narrow(nc.vector.tensor_copy, 1, slice(0, T))
+        low_plane(1)
+        pair_up(0, left)
+        pair_up(0, right)
+        values = [gather_pairs(0, j) for j in range(2)]
+        narrow(nc.scalar.copy, 2, slice(0, T))
+        high_plane(2)
+        for j in range(2):
+            add_two(0, j, values[j], every)
+        narrow(nc.vector.tensor_copy, 3, left)
+        narrow(nc.scalar.copy, 3, right)
+        pair_up(1, left)
+        high_plane(3)
+        pair_up(1, right)
+        values = [gather_pairs(1, j) for j in range(2)]
+        add_two(1, 0, values[0], every)
+        for h in range(HALVES):
+            add_two(1, 1, values[1], halves[h])
+        grouped1 = []
+        for h in range(HALVES):
+            grouped = keep.tile([P, HALF, 2, 2], BF16, name="grouped1_%d" % h, align_bytes=64)
+            first, second = [
+                partial[j][:, :, 2 * h * HALF : 2 * (h + 1) * HALF].rearrange("p u (v e) -> p v u e", e=2)
+                for j in range(2)
+            ]
+            nc.vector.tensor_tensor(grouped[:], first, second, add)
+            grouped1.append(grouped)
+
+        pairs_low = placed([P, HALVES, P, 2], BF16, "pairs_low", 0)
+        nc.scalar.copy(pairs_low[:], sums_low[:].rearrange("v h e p -> v h p e"))
+        pairs_high = keep.tile([P, HALVES, P, 2], BF16, name="pairs_high")
+        for h in range(HALVES):
+            nc.scalar.copy(pairs_high[:, h], sums_high[h][:].rearrange("v e p -> v p e"))
+        for u, pairs in enumerate((pairs_low, pairs_high)):
             for h in range(HALVES):
-                nc.tensor.transpose(turned0[:, u, h * HALF : (h + 1) * HALF], words[:, h, :], late_identity[:])
+                nc.tensor.transpose(
+                    turned[h][:, u, :], pairs[:, h].rearrange("v p e -> v (p e)").bitcast(F32), identity[:]
+                )
+        grouped0 = [keep.tile([P, HALF * PACK], BF16, name="grouped0_%d" % h, align_bytes=64) for h in range(HALVES)]
         for h in range(HALVES):
-            nc.tensor.transpose(turned1[h][:, 0, :], words10[h][:, 0, :], identity[:])
-            nc.tensor.transpose(turned1[h][:, 1, :], words11[h][:, 0, :], identity[:])
-        grouped0 = interleave(nc.scalar.copy, turned0[:], "grouped0")
-        copies = [nc.scalar.copy, nc.vector.tensor_copy]
-        grouped = [interleave(copies[h], turned1[h][:], "grouped1_%d" % h) for h in range(HALVES)]
-        codes0 = keep.tile([P, V], U32, name="codes0", align_bytes=64)
-        plane0 = keep.tile([P, V], U8, name="plane0", align_bytes=64)
-        quantise(grouped0, codes0, plane0)
-        for h in range(HALVES):
-            grouped1 = grouped[h]
-            codes1 = keep.tile([P, HALF], U32, name="codes1_%d" % h, align_bytes=64)
-            plane1 = keep.tile([P, HALF], U8, name="plane1_%d" % h, align_bytes=64)
-            quantise(grouped1, codes1, plane1)
-            acc = psum.tile([N, HALF], F32, name="acc_%d" % h, tag=("bank_b", "bank_c0")[h])
-            cols = slice(h * HALF, (h + 1) * HALF)
-            nc.tensor.matmul_mx(
-                out=acc[:], lhsT=w_codes[:, 0, :].bitcast(FP8X4), lhsT_scale=w_plane[:, 0, :],
-                rhs=codes0[:, cols].bitcast(FP8X4), rhs_scale=plane0[:, cols], start=True, stop=False,
+            nc.scalar.copy(
+                grouped0[h][:].bitcast(F32).rearrange("p (v u) -> p v u", u=2),
+                turned[h][:].rearrange("p u v -> p v u"),
             )
+
+        codes0 = [placed([P, HALF], U32, "codes0_%d" % h, 2 * T + 8 * HALF * h) for h in range(HALVES)]
+        plane0 = [placed([P, HALF], U8, "plane0_%d" % h, 2 * T + 8 * HALF * h + 4 * HALF) for h in range(HALVES)]
+        codes1 = [keep.tile([P, HALF], U32, name="codes1_%d" % h, align_bytes=64) for h in range(HALVES)]
+        plane1 = [keep.tile([P, HALF], U8, name="plane1_%d" % h, align_bytes=64) for h in range(HALVES)]
+
+        def quantise(codes, plane, values):
+            nc.vector.quantize_mx(out=codes[:].bitcast(FP8X4), scales=plane[:], in_=values)
+
+        def multiply(h, a, codes, plane, start):
             nc.tensor.matmul_mx(
-                out=acc[:], lhsT=w_codes[:, 1, :].bitcast(FP8X4), lhsT_scale=w_plane[:, 1, :],
-                rhs=codes1[:].bitcast(FP8X4), rhs_scale=plane1[:], start=False, stop=True,
+                out=acc[h][:], lhsT=w_codes[:, a, :].bitcast(FP8X4), lhsT_scale=w_plane[:, a, :],
+                rhs=codes.bitcast(FP8X4), rhs_scale=plane, start=start, stop=not start,
             )
+
+        def finish(h):
             result = keep.tile([N, HALF], F32, name="result_%d" % h)
-            nc.scalar.activation(result[:], acc[:], ACT.Silu, bias=bias[:])
-            nc.sync.dma_start(out[:, cols], result[:])
+            nc.scalar.activation(result[:], acc[h][:], ACT.Silu, bias=bias[:])
+            nc.sync.dma_start(out[:, halves[h]], result[:])
+
+        for h in range(HALVES):
+            quantise(codes1[h], plane1[h], grouped1[h][:].rearrange("p v u e -> p (v u e)"))
+            multiply(h, 1, codes1[h][:], plane1[h][:], True)
+        for h in range(HALVES):
+            quantise(codes0[h], plane0[h], grouped0[h][:])
+            multiply(h, 0, codes0[h][:], plane0[h][:], False)
+            finish(h)

@@ -46,8 +46,9 @@ def tile_picked_hash_lin_silu_sub_l_kernel(tc, xT, w_words, w_scales, b, offs, o
         nc.sync.dma_start(single[1][:], rows[0, :, 1, :])
         nc.sync.dma_start(double[0][:, :, left], rows[1, :, 0:2, left])
         nc.sync.dma_start(double[0][:, :, right], rows[1, :, 0:2, right])
-        nc.sync.dma_start(single[2][:], rows[0, :, 2, :])
-        nc.sync.dma_start(single[3][:], rows[0, :, 3, :])
+        for t in (2, 3):
+            for cols in (left, right):
+                nc.sync.dma_start(single[t][:, cols], rows[0, :, t, cols])
         nc.sync.dma_start(double[1][:, :, left], rows[1, :, 2:4, left])
         nc.sync.dma_start(double[1][:, :, right], rows[1, :, 2:4, right])
 
@@ -152,11 +153,12 @@ def tile_picked_hash_lin_silu_sub_l_kernel(tc, xT, w_words, w_scales, b, offs, o
         pair_up(0, left)
         pair_up(0, right)
         values = [gather_pairs(0, j) for j in range(2)]
-        narrow(nc.scalar.copy, 2, slice(0, T))
+        narrow(nc.gpsimd.tensor_copy, 2, left)
+        narrow(nc.gpsimd.tensor_copy, 2, right)
         high_plane(2)
         for j in range(2):
             add_two(0, j, values[j], every)
-        narrow(nc.vector.tensor_copy, 3, left)
+        narrow(nc.gpsimd.tensor_copy, 3, left)
         narrow(nc.scalar.copy, 3, right)
         pair_up(1, left)
         high_plane(3)

from contextlib import ExitStack

import concourse.mybir as mybir
from concourse.masks import make_identity

K, T, D, V, N = 1024, 1024, 4, 256, 128
FLOPS = 2 * K * N * V

F32 = mybir.dt.float32
BF16 = mybir.dt.bfloat16
I32 = mybir.dt.int32
U32 = mybir.dt.uint32
U16 = mybir.dt.uint16
U8 = mybir.dt.uint8
FP8X4 = mybir.dt.float8_e4m3fn_x4
ACT = mybir.ActivationFunctionType

P = 128
PACK = 4
PASSES = K // (P * PACK)
HALF = 128
HALVES = V // HALF
GROUP = 16


def tile_picked_hash_lin_silu_sub_l_kernel(tc, xT, w_words, w_scales, b, offs, out):
    nc = tc.nc
    add = mybir.AluOpType.add
    with ExitStack() as ctx:
        keep = ctx.enter_context(tc.tile_pool(name="keep", bufs=1))
        shared = ctx.enter_context(tc.tile_pool(name="shared", bufs=1))
        psum = ctx.enter_context(tc.psum_pool(name="psum", bufs=1))

        def placed(shape, dtype, name, at):
            return shared.tile(shape, dtype, name=name, offset=at, align_bytes=64)

        offsets = keep.tile([P, D * V // GROUP], U16, name="offsets")
        rows = xT.rearrange("(a p t) n -> a p t n", p=P, t=PACK)
        left, right = slice(0, T // 2), slice(T // 2, T)
        most, rest = slice(0, 3 * T // 4), slice(3 * T // 4, T)
        single = [keep.tile([P, T], F32, name="single_%d" % t) for t in range(PACK)]
        double = [keep.tile([P, 2, T], F32, name="double_%d" % u) for u in range(2)]
        nc.sync.dma_start(single[0][:, most], rows[0, :, 0, most])
        nc.sync.dma_start(offsets[:], offs)
        nc.sync.dma_start(single[0][:, rest], rows[0, :, 0, rest])
        nc.sync.dma_start(single[1][:], rows[0, :, 1, :])
        nc.sync.dma_start(double[0][:, :, left], rows[1, :, 0:2, left])
        nc.sync.dma_start(double[0][:, :, right], rows[1, :, 0:2, right])
        for t in (2, 3):
            for cols in (left, right):
                nc.sync.dma_start(single[t][:, cols], rows[0, :, t, cols])
        nc.sync.dma_start(double[1][:, :, left], rows[1, :, 2:4, left])
        nc.sync.dma_start(double[1][:, :, right], rows[1, :, 2:4, right])

        w_codes = keep.tile([P, PASSES, N], U32, name="w_codes", align_bytes=64)
        w_plane = keep.tile([P, PASSES, N], U8, name="w_plane", align_bytes=64)
        bias = keep.tile([P, 1], F32, name="bias")
        widened = [keep.tile([P, D * V], F32, name="widened_%d" % e) for e in range(2)]
        nc.vector.memset(widened[0][:].bitcast(I32), 0)
        nc.gpsimd.memset(w_plane[:].rearrange("p a m -> p (a m)").bitcast(I32), 0)
        nc.sync.dma_start(
            w_codes[:].bitcast(I32), w_words.rearrange("a p m r -> p a (m r)").bitcast(I32)
        )
        nc.sync.dma_start(bias[:], b)
        for q in range(4):
            nc.sync.dma_start(
                w_plane[32 * q : 32 * q + 4].bitcast(I32),
                w_scales[:, 4 * q : 4 * q + 4, :].rearrange("a r m -> r a m").bitcast(I32),
            )

        identity = keep.tile([P, P], F32, name="identity")
        make_identity(nc, identity[:])
        nc.gpsimd.memset(widened[1][:].bitcast(I32), 0)
        warm_in = keep.tile([P, 1], F32, name="warm_in")
        warm_out = keep.tile([P, 1], F32, name="warm_out")
        nc.vector.memset(warm_in[:], 0.0)
        nc.scalar.activation(warm_out[:], warm_in[:], ACT.Silu)

        def list_slice(first, width):
            return offsets[:, first // GROUP : (first + width) // GROUP]

        small = [keep.tile([P, T], BF16, name="small_%d" % t) for t in range(PACK - 1)]
        small.append(placed([P, T], BF16, "small_last", 0))

        def narrow(copy, t, cols):
            copy(small[t][:, cols], single[t][:, cols])

        def gather_scalar(t, d):
            dest = widened[t % 2]
            nc.scalar.activation(
                dest[:].bitcast(BF16)[:, 2 * d * V + 1 : 2 * (d + 1) * V : 2],
                small[t][:].indirect(list_slice(d * V, V)),
                ACT.Copy,
            )
            return dest[:, d * V : (d + 1) * V]

        def gather_vector(t, d):
            picked = keep.tile([P, V], F32, name="picked_%d" % t)
            nc.vector.tensor_copy(picked[:], single[t][:].indirect(list_slice(d * V, V)))
            return picked[:]

        def add_turned(dest, piece, h, i):
            nc.tensor.matmul(
                dest, lhsT=piece[:, h * HALF : (h + 1) * HALF], rhs=identity[:],
                is_transpose=True, start=(i == 0), stop=(i == D - 1),
            )

        sums_low = psum.tile([P, HALVES, 2, P], F32, name="sums_low")
        sums_high = [psum.tile([P, 2, P], F32, name="sums_high_%d" % h) for h in range(HALVES)]
        turned = [psum.tile([P, 2, HALF], F32, name="turned_%d" % h) for h in range(HALVES)]
        acc = [psum.tile([N, HALF], F32, name="acc_%d" % h) for h in range(HALVES)]

        def low_plane(t):
            pieces = [gather_vector(t, D - 1)] + [gather_scalar(t, d) for d in range(D - 1)]
            for h in range(HALVES):
                for i, piece in enumerate(pieces):
                    add_turned(sums_low[:, h, t, :], piece, h, i)

        def high_plane(t):
            for d in range(D):
                piece = gather_scalar(t, d)
                for h in range(HALVES):
                    add_turned(sums_high[h][:, t - 2, :], piece, h, d)

        paired = [keep.tile([P, T], U32, name="paired_%d" % u) for u in range(2)]
        partial = [placed([P, 2, 2 * V], F32, "partial_%d" % j, 2 * T + j * 16 * V) for j in range(2)]

        def pair_up(u, cols):
            nc.vector.tensor_copy(
                paired[u][:, cols].bitcast(BF16).rearrange("p (n e) -> p n e", e=2),
                double[u][:, :, cols].rearrange("p e n -> p n e"),
            )

        def gather_pairs(u, j):
            words = keep.tile([P, 2 * V], U32, name="words_%d_%d" % (u, j))
            nc.vector.tensor_copy(words[:], paired[u][:].indirect(list_slice(2 * j * V, 2 * V)))
            return words[:].bitcast(BF16)

        def add_two(u, j, values, ids):
            cols = slice(2 * ids.start, 2 * ids.stop)
            nc.vector.tensor_tensor(
                partial[j][:, u, cols], values[:, : 2 * V][:, cols], values[:, 2 * V :][:, cols], add
            )

        every = slice(0, V)
        halves = [slice(h * HALF, (h + 1) * HALF) for h in range(HALVES)]

        narrow(nc.vector.tensor_copy, 0, most)
        narrow(nc.vector.tensor_copy, 0, rest)
        low_plane(0)
        narrow(nc.vector.tensor_copy, 1, slice(0, T))
        low_plane(1)
        pair_up(0, left)
        pair_up(0, right)
        values = [gather_pairs(0, j) for j in range(2)]
        narrow(nc.gpsimd.tensor_copy, 2, left)
        narrow(nc.gpsimd.tensor_copy, 2, right)
        high_plane(2)
        for j in range(2):
            add_two(0, j, values[j], every)
        narrow(nc.gpsimd.tensor_copy, 3, left)
        narrow(nc.scalar.copy, 3, right)
        pair_up(1, left)
        high_plane(3)
        pair_up(1, right)
        values = [gather_pairs(1, j) for j in range(2)]
        add_two(1, 0, values[0], every)
        for h in range(HALVES):
            add_two(1, 1, values[1], halves[h])
        grouped1 = []
        for h in range(HALVES):
            grouped = keep.tile([P, HALF, 2, 2], BF16, name="grouped1_%d" % h, align_bytes=64)
            first, second = [
                partial[j][:, :, 2 * h * HALF : 2 * (h + 1) * HALF].rearrange("p u (v e) -> p v u e", e=2)
                for j in range(2)
            ]
            nc.vector.tensor_tensor(grouped[:], first, second, add)
            grouped1.append(grouped)

        pairs_low = placed([P, HALVES, P, 2], BF16, "pairs_low", 0)
        nc.scalar.copy(pairs_low[:], sums_low[:].rearrange("v h e p -> v h p e"))
        pairs_high = keep.tile([P, HALVES, P, 2], BF16, name="pairs_high")
        for h in range(HALVES):
            nc.scalar.copy(pairs_high[:, h], sums_high[h][:].rearrange("v e p -> v p e"))
        for u, pairs in enumerate((pairs_low, pairs_high)):
            for h in range(HALVES):
                nc.tensor.transpose(
                    turned[h][:, u, :], pairs[:, h].rearrange("v p e -> v (p e)").bitcast(F32), identity[:]
                )
        grouped0 = [keep.tile([P, HALF * PACK], BF16, name="grouped0_%d" % h, align_bytes=64) for h in range(HALVES)]
        for h in range(HALVES):
            nc.scalar.copy(
                grouped0[h][:].bitcast(F32).rearrange("p (v u) -> p v u", u=2),
                turned[h][:].rearrange("p u v -> p v u"),
            )

        codes0 = [placed([P, HALF], U32, "codes0_%d" % h, 2 * T + 8 * HALF * h) for h in range(HALVES)]
        plane0 = [placed([P, HALF], U8, "plane0_%d" % h, 2 * T + 8 * HALF * h + 4 * HALF) for h in range(HALVES)]
        codes1 = [keep.tile([P, HALF], U32, name="codes1_%d" % h, align_bytes=64) for h in range(HALVES)]
        plane1 = [keep.tile([P, HALF], U8, name="plane1_%d" % h, align_bytes=64) for h in range(HALVES)]

        def quantise(codes, plane, values):
            nc.vector.quantize_mx(out=codes[:].bitcast(FP8X4), scales=plane[:], in_=values)

        def multiply(h, a, codes, plane, start):
            nc.tensor.matmul_mx(
                out=acc[h][:], lhsT=w_codes[:, a, :].bitcast(FP8X4), lhsT_scale=w_plane[:, a, :],
                rhs=codes.bitcast(FP8X4), rhs_scale=plane, start=start, stop=not start,
            )

        def finish(h):
            result = keep.tile([N, HALF], F32, name="result_%d" % h)
            nc.scalar.activation(result[:], acc[h][:], ACT.Silu, bias=bias[:])
            nc.sync.dma_start(out[:, halves[h]], result[:])

        for h in range(HALVES):
            quantise(codes1[h], plane1[h], grouped1[h][:].rearrange("p v u e -> p (v u e)"))
            multiply(h, 1, codes1[h][:], plane1[h][:], True)
        for h in range(HALVES):
            quantise(codes0[h], plane0[h], grouped0[h][:])
            multiply(h, 0, codes0[h][:], plane0[h][:], False)
            finish(h)
